import numpy as np
import ml_dtypes


def mxq(x, axis, fmt="e4m3"):
    dtype, down = {"e4m3": (ml_dtypes.float8_e4m3fn, 7), "e5m2": (ml_dtypes.float8_e5m2, 14)}[fmt]
    v = np.moveaxis(np.asarray(x, np.float32).astype(ml_dtypes.bfloat16).astype(np.float64), axis, -1)
    blocks = v.reshape(v.shape[:-1] + (-1, 32))
    amax = np.abs(blocks).max(-1, keepdims=True)
    byte = np.maximum(np.where(amax > 0, np.frexp(amax)[1] - 1 + 127, 0) - down, 1)
    scale = np.exp2(byte - 127.0)
    codes = (blocks / scale).astype(np.float32).astype(dtype).astype(np.float64)
    return np.moveaxis((codes * scale).reshape(v.shape), -1, axis)


WIDE = False


def mx_kscale(k):
    if not WIDE:
        return np.ones(k)
    levels = np.array([10, -10, 5, -5, 0])
    if k % 512:
        return np.exp2(np.random.permutation(np.resize(levels, k // 32))).repeat(32)
    a = np.empty((k // 512, 16))
    for p in range(k // 512):
        a[p, :8] = np.random.permutation(np.resize(levels, 8))
        for g in range(8):
            far = levels[np.abs(levels - a[p, g]) >= 10]
            a[p, g + 8] = far[np.random.randint(len(far))]
    return np.exp2(a.ravel()).repeat(32)


BF16 = ml_dtypes.bfloat16


def bf(x):
    return np.asarray(x, np.float32).astype(BF16)


def f64(x):
    return np.asarray(x).astype(np.float64)

def planes(Y):
    n, m = Y.shape
    b = f64(bf(Y)).reshape(n // 32, 32, m)
    amax = np.abs(b).max(1)
    byte = np.clip(np.where(amax > 0, np.frexp(amax)[1] - 1 + 127 - 7, 1), 1, 254)
    codes = (b * np.exp2(127.0 - byte)[:, None, :]).reshape(n, m).astype(np.float32).astype(ml_dtypes.float8_e4m3fn).view(np.uint8)
    words = codes.reshape(n // 512, 128, 4, m).transpose(0, 1, 3, 2)
    return np.ascontiguousarray(words), np.ascontiguousarray(byte.astype(np.uint8).reshape(n // 512, 16, m))


B, S, N, P = 2, 1024, 512, 512


def two_sided_decay(t, lf, lb):
    d = t[:, :, None] - t[:, None, :]
    fwd = -lf[:, None, None] * d
    bwd = lb[:, None, None] * d
    return np.exp(np.where(d >= 0, fwd, bwd))


def setup_inputs():
    s, u = mx_kscale(N), mx_kscale(S)
    return {"c": bf(np.random.standard_normal((B, S, N)) * s),
            "b": bf(np.random.standard_normal((B, S, N)) / np.sqrt(N) / s),
            "x": bf(np.random.standard_normal((B, S, P)) / u[:, None]),
            "t": bf(np.random.uniform(0.0, 4.0, (B, S))),
            "dt": bf(np.random.uniform(0.5, 1.5, (B, S)) * u),
            "lf": bf(np.random.uniform(0.3, 1.0, (B,))),
            "lb": bf(np.random.uniform(1.5, 3.0, (B,)))}


def core(c, b, x, t, dt, lf, lb):
    cq = mxq(f64(c), 2, "e4m3")
    bq = mxq(f64(b), 2, "e4m3")
    s = cq @ bq.transpose(0, 2, 1)
    e = two_sided_decay(f64(t), f64(lf), f64(lb))
    m = s * e * f64(dt)[:, None, :]
    return (mxq(m, 2, "e4m3") @ mxq(f64(x), 1, "e4m3")) / np.sqrt(S)


def reference(c, b, x, t, dt, lf, lb):
    R_out = core(c, b, x, t, dt, lf, lb)
    words, scales = planes(np.moveaxis(R_out, 2, 0).reshape(512, -1))
    return R_out, words, scales

@@ -1,0 +1,433 @@
+import math
+from contextlib import ExitStack
+
+import concourse.mybir as mybir
+from concourse.masks import make_identity
+
+B, S, N, P = 2, 1024, 512, 512
+FLOPS = 2 * B * S * S * N + 2 * B * S * S * P
+
+F32 = mybir.dt.float32
+BF16 = mybir.dt.bfloat16
+I32 = mybir.dt.int32
+U32 = mybir.dt.uint32
+U8 = mybir.dt.uint8
+FP8X4 = mybir.dt.float8_e4m3fn_x4
+ALU = mybir.AluOpType
+ACT = mybir.ActivationFunctionType
+
+PART = 128
+PACK = 4
+KP = PART * PACK
+HALVES = B * S // KP
+UNITS = B * S // PART
+S_BANKS = 4
+ACT_BANKS = 3
+E_SLOTS = 6
+ARG_LEAD = 12
+X_SPLIT = 4
+OUT_SCALE = 1.0 / math.sqrt(S)
+
+
+def tile_irregulartwosidedssdsmoother_x1_kernel(tc, c, b, x, t, dt, lf, lb, out_0, out_1, out_2):
+    nc = tc.nc
+    with ExitStack() as ctx:
+        sb = ctx.enter_context(tc.tile_pool(name="sb", bufs=1))
+        ps = ctx.enter_context(tc.psum_pool(name="ps", bufs=1))
+        ctx.enter_context(tc.manual_schedule())
+
+        def sbuf(shape, dtype, tag):
+            return sb.tile(shape, dtype, name=tag, tag=tag, align_bytes=64)
+
+        banks_taken = []
+
+        def act_bank():
+            tag = "act%d" % (len(banks_taken) % ACT_BANKS)
+            banks_taken.append(tag)
+            return ps.tile([PART, KP], F32, name=tag, tag=tag)
+
+        t_sb = sbuf([PART, HALVES, PACK], BF16, "t_sb")
+        dt_sb = sbuf([PART, HALVES, PACK], BF16, "dt_sb")
+        lf_sb = sbuf([PART, B], BF16, "lf_sb")
+        lb_sb = sbuf([PART, B], BF16, "lb_sb")
+        nc.sync.dma_start(out=t_sb[:], in_=t.rearrange("n (g p j) -> p (n g) j", g=2, j=PACK))
+        nc.scalar.dma_start(out=dt_sb[:], in_=dt.rearrange("n (g p j) -> p (n g) j", g=2, j=PACK))
+        nc.sync.dma_start(out=lf_sb[:], in_=lf.partition_broadcast(PART))
+        nc.sync.dma_start(out=lb_sb[:], in_=lb.partition_broadcast(PART))
+
+        raw = {}
+
+        def load(which, h):
+            n, g = divmod(h, 2)
+            rows = {"b": b, "c": c, "x": x}[which][n, g * KP:(g + 1) * KP, :]
+            raw[which, h] = sbuf([PART, PACK, N], BF16, "raw_%s%d" % (which, h))
+            if which == "c":
+                nc.sync.dma_start(
+                    out=raw[which, h][:].rearrange("p (q r) k -> p q (r k)", r=2),
+                    in_=rows.rearrange("(q p r) k -> p q (r k)", q=2, r=2))
+            else:
+                nc.sync.dma_start(out=raw[which, h][:], in_=rows.rearrange("(p j) k -> p j k", j=PACK))
+
+        for which, h in [("b", 0), ("x", 0), ("c", 0), ("b", 1), ("x", 1), ("c", 1),
+                         ("b", 2), ("b", 3), ("x", 2), ("c", 2), ("x", 3), ("c", 3)]:
+            load(which, h)
+
+        ident = sbuf([PART, PART], F32, "ident")
+        make_identity(nc, ident[:])
+
+        one = sbuf([PART, 1], F32, "one")
+        warm = sbuf([PART, 1], F32, "warm")
+        nc.vector.memset(one[:], 1.0)
+        nc.scalar.activation(out=warm[:], in_=one[:], func=ACT.Ln)
+
+        COLS = HALVES * PACK
+        fwd = sbuf([PART, COLS], F32, "fwd")
+        bwd = sbuf([PART, COLS], F32, "bwd")
+        both = sbuf([PART, COLS], F32, "both")
+        t_flat = t_sb[:].rearrange("p h j -> p (h j)")
+        dt32 = sbuf([PART, COLS], F32, "dt32")
+        mant = sbuf([PART, COLS], I32, "mant")
+        expo_i = sbuf([PART, COLS], I32, "expo_i")
+        sign = sbuf([PART, COLS], I32, "sign")
+        ln_mant = sbuf([PART, COLS], F32, "ln_mant")
+        warm2 = sbuf([PART, 1], F32, "warm2")
+        expo = sbuf([PART, COLS], F32, "expo")
+        k1 = sbuf([PART, COLS], F32, "k1")
+        k2 = sbuf([PART, COLS], F32, "k2")
+        k3 = sbuf([PART, COLS], F32, "k3")
+        k4 = sbuf([PART, COLS], F32, "k4")
+        bias = sbuf([PART, COLS], F32, "bias")
+        bits = dt32[:].bitcast(I32)
+
+        def rates(n):
+            cols = slice(n * 8, n * 8 + 8)
+            nc.vector.tensor_scalar(out=bwd[:, cols], in0=t_flat[:, cols], scalar1=lb_sb[:, n:n + 1],
+                                    scalar2=None, op0=ALU.mult)
+            nc.vector.tensor_scalar(out=fwd[:, cols], in0=t_flat[:, cols], scalar1=lf_sb[:, n:n + 1],
+                                    scalar2=-1.0, op0=ALU.mult, op1=ALU.mult)
+
+        nc.vector.tensor_copy(out=dt32[:], in_=dt_sb[:].rearrange("p h j -> p (h j)"))
+        rates(0)
+        rates(1)
+        nc.vector.tensor_scalar(out=mant[:], in0=bits, scalar1=0x007FFFFF, scalar2=0x3F800000,
+                                op0=ALU.bitwise_and, op1=ALU.bitwise_or)
+        nc.vector.tensor_scalar(out=expo_i[:], in0=bits, scalar1=23, scalar2=0xFF,
+                                op0=ALU.logical_shift_right, op1=ALU.bitwise_and)
+        nc.vector.tensor_scalar(out=sign[:], in0=bits, scalar1=-0x80000000, scalar2=0x3F800000,
+                                op0=ALU.bitwise_and, op1=ALU.bitwise_or)
+        nc.vector.tensor_tensor(out=both[:], in0=bwd[:], in1=fwd[:], op=ALU.subtract)
+        nc.scalar.activation(out=ln_mant[:], in_=mant[:].bitcast(F32), func=ACT.Ln)
+        nc.scalar.activation(out=warm2[:], in_=one[:], func=ACT.Exp)
+        nc.vector.tensor_copy(out=expo[:], in_=expo_i[:])
+        nc.vector.tensor_tensor(out=k4[:], in0=ln_mant[:], in1=bwd[:], op=ALU.subtract)
+        nc.vector.tensor_scalar(out=k1[:], in0=expo[:], scalar1=-127.0, scalar2=math.log(2.0),
+                                op0=ALU.add, op1=ALU.mult)
+        nc.vector.tensor_scalar(out=k2[:], in0=expo[:], scalar1=0.0, scalar2=-1e30,
+                                op0=ALU.is_equal, op1=ALU.mult)
+
+        def bias_b():
+            nc.vector.tensor_tensor(out=k3[:], in0=k1[:], in1=k2[:], op=ALU.add)
+
+        def bias_c():
+            nc.vector.tensor_tensor(out=bias[:], in0=k3[:], in1=k4[:], op=ALU.add)
+
+        fwd_row, bwd_bank, bwd_row = {}, {}, {}
+
+        def spread(bank, col_tile, h):
+            for j in range(PACK):
+                col = h * PACK + j
+                nc.tensor.transpose(bank[:, j * PART:(j + 1) * PART],
+                                    col_tile[:, col:col + 1].to_broadcast([PART, PART]), ident[:])
+
+        def spread_fwd(h):
+            fwd_row[h] = ps.tile([PART, KP], F32, name="fwd_row", tag="fwd_row")
+            spread(fwd_row[h], fwd, h)
+
+        def spread_bwd(h):
+            bwd_bank[h] = act_bank()
+            spread(bwd_bank[h], bwd, h)
+
+        def copy_bwd(h, eng):
+            bwd_row[h] = sbuf([PART, KP], F32, "bwd_row%d" % h)
+            src = bwd_bank[h][:].rearrange("p (j m) -> p m j", j=PACK)
+            dst = bwd_row[h][:].rearrange("p (m j) -> p m j", j=PACK)
+            if eng == "v":
+                nc.vector.tensor_copy(out=dst, in_=src)
+            else:
+                nc.scalar.copy(out=dst, in_=src)
+
+        turned, grouped, codes, scales = {}, {}, {}, {}
+
+        def new_grouped(key):
+            if key[0] == "x":
+                tag = "grouped_x%d" % key[1]
+            else:
+                tag = "grouped%d" % (len([q for q in grouped if q[0] != "x"]) % 3)
+            grouped[key] = sbuf([PART, KP * PACK], BF16, tag)
+
+        def turn(which, h, q):
+            words = raw[which, h][:].rearrange("p s k -> p (s k)").bitcast(F32)
+            bank = act_bank()
+            turned[which, h, q] = bank
+            for r in range(2):
+                for u in range(2):
+                    w0 = (2 * q + r) * 256 + u
+                    nc.tensor.transpose(bank[:, (2 * r + u) * PART:(2 * r + u + 1) * PART],
+                                        words[:, w0:(2 * q + r + 1) * 256:2], ident[:])
+
+        def copy_turned(which, h, q):
+            if q == 0:
+                new_grouped((which, h))
+            dst = grouped[which, h][:, q * 1024:(q + 1) * 1024].bitcast(F32)
+            bank = turned[which, h, q]
+            if which == "c":
+                nc.scalar.copy(out=dst.rearrange("p (m r u) -> p m r u", r=2, u=2),
+                               in_=bank[:].rearrange("p (r u m) -> p m r u", r=2, u=2))
+            else:
+                nc.scalar.copy(out=dst.rearrange("p (r m u) -> p r m u", r=2, u=2),
+                               in_=bank[:].rearrange("p (r u m) -> p r m u", r=2, u=2))
+
+
+        def interleave_x(h):
+            new_grouped(("x", h))
+            dst = grouped["x", h][:].rearrange("p (s m j) -> p s m j", s=PACK, j=PACK)
+            src = raw["x", h][:].rearrange("p j (m s) -> p s m j", s=PACK)
+            width = PART // X_SPLIT
+            sgn = sign[:].bitcast(F32)[:, h * PACK:(h + 1) * PACK].unsqueeze(1).to_broadcast([PART, width, PACK])
+            for s in range(PACK):
+                for m0 in range(0, PART, width):
+                    nc.gpsimd.tensor_tensor(out=dst[:, s, m0:m0 + width, :], in0=src[:, s, m0:m0 + width, :],
+                                            in1=sgn, op=ALU.mult)
+
+        def quantize(which, h):
+            codes[which, h] = sbuf([PART, KP], U32, "codes_%s%d" % (which, h))
+            scales[which, h] = sbuf([PART, KP], U8, "scales_%s%d" % (which, h))
+            nc.vector.quantize_mx(out=codes[which, h][:].bitcast(FP8X4), scales=scales[which, h][:],
+                                  in_=grouped[which, h][:])
+
+        decay = {}
+
+        def arg(a):
+            h, rest = divmod(a, 8)
+            g, j = divmod(rest, PACK)
+            if j == 0:
+                decay[h, g] = sbuf([PART, PACK, KP], F32, "decay%d" % ((2 * h + g) % E_SLOTS))
+            col = ((h // 2) * 2 + g) * PACK + j
+            nc.vector.scalar_tensor_tensor(
+                out=decay[h, g][:, j, :].rearrange("p (m r) -> p m r", r=PACK),
+                in0=fwd_row[h][:].rearrange("p (r m) -> p m r", r=PACK),
+                scalar=both[:, col:col + 1],
+                in1=bwd_row[h][:].rearrange("p (m r) -> p m r", r=PACK),
+                op0=ALU.add, op1=ALU.min)
+
+        def expo_step(a):
+            h, rest = divmod(a, 8)
+            g, j = divmod(rest, PACK)
+            col = ((h // 2) * 2 + g) * PACK + j
+            nc.scalar.activation(out=decay[h, g][:, j, :], in_=decay[h, g][:, j, :], func=ACT.Exp,
+                                 bias=bias[:, col:col + 1])
+
+        s_bank, m_bf, m_codes, m_scales = {}, {}, {}, {}
+
+        def scores(u, g):
+            h, ib = divmod(u, PACK)
+            hb = (h // 2) * 2 + g
+            tag = "s%d" % ((2 * u + g) % S_BANKS)
+            s_bank[u, g] = ps.tile([PART, KP], F32, name=tag, tag=tag)
+            cols = slice(ib * PART, (ib + 1) * PART)
+            for j in range(PACK):
+                js = slice(j * PART, (j + 1) * PART)
+                nc.tensor.matmul_mx(out=s_bank[u, g][:, js],
+                                    lhsT=codes["b", hb][:, js].bitcast(FP8X4), lhsT_scale=scales["b", hb][:, js],
+                                    rhs=codes["c", h][:, cols].bitcast(FP8X4), rhs_scale=scales["c", h][:, cols],
+                                    start=True, stop=True)
+
+        def weigh(u, g):
+            h, ib = divmod(u, PACK)
+            if g == 0:
+                m_bf[u] = sbuf([PART, 2 * KP], BF16, "m_bf%d" % (u % 4))
+            nc.vector.tensor_tensor(
+                out=m_bf[u][:, g * KP:(g + 1) * KP].rearrange("p (c i j) -> p c j i", i=4, j=PACK),
+                in0=s_bank[u, g][:].rearrange("p (j c i) -> p c j i", j=PACK, i=4),
+                in1=decay[h, g][:, :, ib * PART:(ib + 1) * PART].rearrange("p j (c i) -> p c j i", i=4),
+                op=ALU.mult)
+
+        def quantize_m(u):
+            m_codes[u] = sbuf([PART, 2 * PART], U32, "m_codes%d" % (u % 4))
+            m_scales[u] = sbuf([PART, 2 * PART], U8, "m_scales%d" % (u % 4))
+            nc.vector.quantize_mx(out=m_codes[u][:].bitcast(FP8X4), scales=m_scales[u][:], in_=m_bf[u][:])
+
+        row_bank, col_bank = {}, {}
+        y_codes = sbuf([PART, B * S], U32, "y_codes")
+        y_scales = sbuf([PART, B * S], U8, "y_scales")
+
+        def out_rows(u):
+            n = u // 8
+            row_bank[u] = act_bank()
+            for g in range(2):
+                ms = slice(g * PART, (g + 1) * PART)
+                nc.tensor.matmul_mx(out=row_bank[u][:],
+                                    lhsT=m_codes[u][:, ms].bitcast(FP8X4), lhsT_scale=m_scales[u][:, ms],
+                                    rhs=codes["x", 2 * n + g][:].bitcast(FP8X4), rhs_scale=scales["x", 2 * n + g][:],
+                                    start=(g == 0), stop=(g == 1))
+
+        def out_cols(u):
+            n = u // 8
+            col_bank[u] = act_bank()
+            for s in range(PACK):
+                cs = slice(s * PART, (s + 1) * PART)
+                for g in range(2):
+                    ms = slice(g * PART, (g + 1) * PART)
+                    nc.tensor.matmul_mx(out=col_bank[u][:, cs],
+                                        lhsT=codes["x", 2 * n + g][:, cs].bitcast(FP8X4),
+                                        lhsT_scale=scales["x", 2 * n + g][:, cs],
+                                        rhs=m_codes[u][:, ms].bitcast(FP8X4), rhs_scale=m_scales[u][:, ms],
+                                        start=(g == 0), stop=(g == 1))
+
+        out_flat = out_0.rearrange("n i w -> (n i) w")
+
+        def store_rows(u, eng):
+            y = sbuf([PART, P], F32, "y%d" % (u % 6))
+            dst = y[:].rearrange("p (m s) -> p m s", s=PACK)
+            src = row_bank[u][:].rearrange("p (s m) -> p m s", s=PACK)
+            if eng == "v":
+                nc.vector.tensor_scalar(out=dst, in0=src, scalar1=OUT_SCALE, scalar2=None, op0=ALU.mult)
+            else:
+                nc.scalar.activation(out=dst, in_=src, func=ACT.Copy, scale=OUT_SCALE)
+            nc.sync.dma_start(out=out_flat[u * PART:(u + 1) * PART, :], in_=y[:])
+
+        y_bf = sbuf([PART, B * S * PACK], BF16, "y_bf")
+
+        def copy_cols(u):
+            nc.scalar.activation(out=y_bf[:, u * KP:(u + 1) * KP].rearrange("p (i s) -> p i s", s=PACK),
+                                 in_=col_bank[u][:].rearrange("p (s i) -> p i s", s=PACK),
+                                 func=ACT.Copy, scale=OUT_SCALE)
+
+        def quantize_y(u0, u1):
+            cols = slice(u0 * PART, u1 * PART)
+            nc.vector.quantize_mx(out=y_codes[:, cols].bitcast(FP8X4), scales=y_scales[:, cols],
+                                  in_=y_bf[:, u0 * KP:u1 * KP])
+
+        words_out = out_1.rearrange("g p m t -> p (g m t)").bitcast(I32)
+        scales_out = out_2.rearrange("g q m -> (g q) m").bitcast(I32)
+
+        def store_words(u0, u1):
+            cols = slice(u0 * PART, u1 * PART)
+            nc.sync.dma_start(out=words_out[:, cols], in_=y_codes[:, cols].bitcast(I32))
+
+        def store_scales(u0, u1, engines):
+            cols = slice(u0 * 32, u1 * 32)
+            for q in range(4):
+                engines[q % len(engines)].dma_start(out=scales_out[4 * q:4 * q + 4, cols],
+                                                    in_=y_scales[:].bitcast(I32)[32 * q:32 * q + 4, cols])
+
+        spread_bwd(0)
+        spread_fwd(0)
+        bias_b()
+        copy_bwd(0, "v")
+        bias_c()
+        interleave_x(0)
+        interleave_x(1)
+        turn("b", 0, 0)
+        turn("b", 0, 1)
+        arg(0)
+        arg(1)
+        copy_turned("b", 0, 0)
+        turn("c", 0, 0)
+        expo_step(0)
+        copy_turned("b", 0, 1)
+        turn("c", 0, 1)
+        arg(2)
+        expo_step(1)
+        arg(3)
+        copy_turned("c", 0, 0)
+        turn("b", 1, 0)
+        arg(4)
+        copy_turned("c", 0, 1)
+        spread_bwd(1)
+        quantize("b", 0)
+        arg(5)
+        expo_step(2)
+        copy_turned("b", 1, 0)
+        turn("b", 1, 1)
+        arg(6)
+        copy_bwd(1, "a")
+        arg(7)
+        spread_fwd(1)
+        quantize("c", 0)
+        copy_turned("b", 1, 1)
+        expo_step(3)
+        expo_step(4)
+        expo_step(5)
+        scores(0, 0)
+        quantize("x", 0)
+        arg(8)
+        quantize("b", 1)
+        expo_step(6)
+        expo_step(7)
+        scores(0, 1)
+        for a in range(9, ARG_LEAD):
+            arg(a)
+        interleave_x(2)
+        interleave_x(3)
+
+        prep = {0: ("c", 1), 2: ("b", 2), 3: ("b", 3), 4: ("c", 2), 7: ("c", 3)}
+        x_quant = {0: 1, 6: 2, 7: 3}
+        arg_counts = [1, 1, 2, 2, 2, 2, 2, 2, 1, 2, 2, 1, 0, 0, 0, 0]
+        y_quant = {11: (0, 4), 12: (4, 8), 13: (8, 12), 15: (12, 14)}
+        next_arg = ARG_LEAD
+        next_exp = 8
+        last = UNITS - 1
+        for u in range(UNITS):
+            for k in range(3):
+                if next_exp < next_arg:
+                    expo_step(next_exp)
+                    next_exp += 1
+            todo = list(range(next_arg, next_arg + arg_counts[u]))
+            next_arg += arg_counts[u]
+            new_half = next_arg % 8 == 0 and next_arg < 8 * HALVES and todo
+            if todo and todo[0] % 8 == 0:
+                spread_fwd(todo[0] // 8)
+            if u < last:
+                scores(u + 1, 0)
+                scores(u + 1, 1)
+            if u >= 1:
+                out_rows(u - 1)
+                out_cols(u - 1)
+                store_rows(u - 1, "a")
+            weigh(u, 0)
+            weigh(u, 1)
+            if u >= 1:
+                copy_cols(u - 1)
+            if u in prep:
+                turn(prep[u][0], prep[u][1], 0)
+                copy_turned(prep[u][0], prep[u][1], 0)
+                turn(prep[u][0], prep[u][1], 1)
+            if new_half:
+                spread_bwd(next_arg // 8)
+            if todo:
+                arg(todo[0])
+            if u in y_quant:
+                quantize_y(*y_quant[u])
+                store_words(*y_quant[u])
+            quantize_m(u)
+            if len(todo) > 1:
+                arg(todo[1])
+            if u in x_quant:
+                quantize("x", x_quant[u])
+            if u - 1 in prep:
+                quantize(prep[u - 1][0], prep[u - 1][1])
+            if u in prep:
+                copy_turned(prep[u][0], prep[u][1], 1)
+            if new_half:
+                copy_bwd(next_arg // 8, "a")
+            if u == 13:
+                store_scales(0, 12, [nc.sync])
+        out_cols(last)
+        out_rows(last)
+        quantize_y(last - 1, last)
+        copy_cols(last)
+        store_rows(last, "v")
+        quantize_y(last, UNITS)
+        store_words(last - 1, UNITS)
+        store_scales(12, UNITS, [nc.scalar, nc.sync])

@@ -24,8 +24,7 @@ UNITS = B * S // PART
 S_BANKS = 4
 ACT_BANKS = 3
 E_SLOTS = 6
-ARG_LEAD = 12
-X_SPLIT = 4
+ARG_LEAD = 8
 OUT_SCALE = 1.0 / math.sqrt(S)
 
 
@@ -188,16 +187,21 @@ def tile_irregulartwosidedssdsmoother_x1_kernel(tc, c, b, x, t, dt, lf, lb, out_
                                in_=bank[:].rearrange("p (r u m) -> p r m u", r=2, u=2))
 
 
-        def interleave_x(h):
-            new_grouped(("x", h))
-            dst = grouped["x", h][:].rearrange("p (s m j) -> p s m j", s=PACK, j=PACK)
-            src = raw["x", h][:].rearrange("p j (m s) -> p s m j", s=PACK)
-            width = PART // X_SPLIT
-            sgn = sign[:].bitcast(F32)[:, h * PACK:(h + 1) * PACK].unsqueeze(1).to_broadcast([PART, width, PACK])
-            for s in range(PACK):
-                for m0 in range(0, PART, width):
-                    nc.gpsimd.tensor_tensor(out=dst[:, s, m0:m0 + width, :], in0=src[:, s, m0:m0 + width, :],
-                                            in1=sgn, op=ALU.mult)
+        def sign_x(h, j):
+            col = h * PACK + j
+            nc.vector.tensor_scalar(out=raw["x", h][:, j, :], in0=raw["x", h][:, j, :],
+                                    scalar1=sign[:].bitcast(F32)[:, col:col + 1], scalar2=None, op0=ALU.mult)
+
+        def interleave_x(h, half, eng):
+            if half == 0:
+                new_grouped(("x", h))
+            dst = grouped["x", h][:].rearrange("p (s c m j) -> p c s m j", s=PACK, m=2, j=PACK)
+            src = raw["x", h][:].rearrange("p j (c m s) -> p c s m j", s=PACK, m=2)
+            cs = slice(half * 32, half * 32 + 32)
+            if eng == "v":
+                nc.vector.tensor_copy(out=dst[:, cs], in_=src[:, cs])
+            else:
+                nc.scalar.copy(out=dst[:, cs], in_=src[:, cs])
 
         def quantize(which, h):
             codes[which, h] = sbuf([PART, KP], U32, "codes_%s%d" % (which, h))
@@ -247,9 +251,9 @@ def tile_irregulartwosidedssdsmoother_x1_kernel(tc, c, b, x, t, dt, lf, lb, out_
             if g == 0:
                 m_bf[u] = sbuf([PART, 2 * KP], BF16, "m_bf%d" % (u % 4))
             nc.vector.tensor_tensor(
-                out=m_bf[u][:, g * KP:(g + 1) * KP].rearrange("p (c i j) -> p c j i", i=4, j=PACK),
-                in0=s_bank[u, g][:].rearrange("p (j c i) -> p c j i", j=PACK, i=4),
-                in1=decay[h, g][:, :, ib * PART:(ib + 1) * PART].rearrange("p j (c i) -> p c j i", i=4),
+                out=m_bf[u][:, g * KP:(g + 1) * KP].rearrange("p (c i j) -> p c j i", i=2, j=PACK),
+                in0=s_bank[u, g][:].rearrange("p (j c i) -> p c j i", j=PACK, i=2),
+                in1=decay[h, g][:, :, ib * PART:(ib + 1) * PART].rearrange("p j (c i) -> p c j i", i=2),
                 op=ALU.mult)
 
         def quantize_m(u):
@@ -326,8 +330,6 @@ def tile_irregulartwosidedssdsmoother_x1_kernel(tc, c, b, x, t, dt, lf, lb, out_
         bias_b()
         copy_bwd(0, "v")
         bias_c()
-        interleave_x(0)
-        interleave_x(1)
         turn("b", 0, 0)
         turn("b", 0, 1)
         arg(0)
@@ -351,29 +353,39 @@ def tile_irregulartwosidedssdsmoother_x1_kernel(tc, c, b, x, t, dt, lf, lb, out_
         copy_turned("b", 1, 0)
         turn("b", 1, 1)
         arg(6)
-        copy_bwd(1, "a")
+        expo_step(3)
         arg(7)
+        copy_turned("b", 1, 1)
         spread_fwd(1)
         quantize("c", 0)
-        copy_turned("b", 1, 1)
-        expo_step(3)
+        copy_bwd(1, "a")
+        turn("c", 1, 0)
+        for j in range(PACK):
+            sign_x(0, j)
+        for j in range(PACK):
+            sign_x(1, j)
         expo_step(4)
         expo_step(5)
         scores(0, 0)
-        quantize("x", 0)
-        arg(8)
+        interleave_x(0, 0, "v")
+        interleave_x(0, 1, "v")
         quantize("b", 1)
         expo_step(6)
         expo_step(7)
         scores(0, 1)
-        for a in range(9, ARG_LEAD):
+        interleave_x(1, 0, "v")
+        quantize("x", 0)
+        interleave_x(1, 1, "v")
+        copy_turned("c", 1, 0)
+        for a in range(8, ARG_LEAD):
             arg(a)
-        interleave_x(2)
-        interleave_x(3)
 
-        prep = {0: ("c", 1), 2: ("b", 2), 3: ("b", 3), 4: ("c", 2), 7: ("c", 3)}
-        x_quant = {0: 1, 6: 2, 7: 3}
-        arg_counts = [1, 1, 2, 2, 2, 2, 2, 2, 1, 2, 2, 1, 0, 0, 0, 0]
+        turns = {0: [("c", 1, 1), ("b", 2, 0)], 1: [("b", 2, 1)], 2: [("b", 3, 0)], 3: [("b", 3, 1)],
+                 4: [("c", 2, 0)], 5: [("c", 2, 1)], 8: [("c", 3, 0)], 9: [("c", 3, 1)]}
+        quants = {0: ("x", 1), 1: ("c", 1), 2: ("b", 2), 4: ("b", 3), 6: ("c", 2), 7: ("x", 2), 8: ("x", 3), 10: ("c", 3)}
+        signs = {3: 2, 5: 3}
+        x_copies = {4: (2, 0), 5: (2, 1), 6: (3, 0), 7: (3, 1)}
+        arg_counts = [2, 3, 3, 2, 2, 2, 2, 2, 2, 2, 2, 0, 0, 0, 0, 0]
         y_quant = {11: (0, 4), 12: (4, 8), 13: (8, 12), 15: (12, 14)}
         next_arg = ARG_LEAD
         next_exp = 8
@@ -386,7 +398,7 @@ def tile_irregulartwosidedssdsmoother_x1_kernel(tc, c, b, x, t, dt, lf, lb, out_
             todo = list(range(next_arg, next_arg + arg_counts[u]))
             next_arg += arg_counts[u]
             new_half = next_arg % 8 == 0 and next_arg < 8 * HALVES and todo
-            if todo and todo[0] % 8 == 0:
+            if todo and todo[0] % 8 == 0 and todo[0] > 8:
                 spread_fwd(todo[0] // 8)
             if u < last:
                 scores(u + 1, 0)
@@ -399,35 +411,34 @@ def tile_irregulartwosidedssdsmoother_x1_kernel(tc, c, b, x, t, dt, lf, lb, out_
             weigh(u, 1)
             if u >= 1:
                 copy_cols(u - 1)
-            if u in prep:
-                turn(prep[u][0], prep[u][1], 0)
-                copy_turned(prep[u][0], prep[u][1], 0)
-                turn(prep[u][0], prep[u][1], 1)
+            for job in turns.get(u, []):
+                turn(*job)
+                copy_turned(*job)
             if new_half:
                 spread_bwd(next_arg // 8)
+                copy_bwd(next_arg // 8, "a")
             if todo:
                 arg(todo[0])
+            if u in signs:
+                for j in range(PACK):
+                    sign_x(signs[u], j)
             if u in y_quant:
                 quantize_y(*y_quant[u])
                 store_words(*y_quant[u])
             quantize_m(u)
-            if len(todo) > 1:
-                arg(todo[1])
-            if u in x_quant:
-                quantize("x", x_quant[u])
-            if u - 1 in prep:
-                quantize(prep[u - 1][0], prep[u - 1][1])
-            if u in prep:
-                copy_turned(prep[u][0], prep[u][1], 1)
-            if new_half:
-                copy_bwd(next_arg // 8, "a")
+            for a in todo[1:]:
+                arg(a)
+            if u in quants:
+                quantize(*quants[u])
+            if u in x_copies:
+                interleave_x(*x_copies[u], "a")
             if u == 13:
                 store_scales(0, 12, [nc.sync])
         out_cols(last)
         out_rows(last)
         quantize_y(last - 1, last)
         copy_cols(last)
-        store_rows(last, "v")
+        store_rows(last, "a")
         quantize_y(last, UNITS)
         store_words(last - 1, UNITS)
         store_scales(12, UNITS, [nc.scalar, nc.sync])

@@ -24,7 +24,7 @@ UNITS = B * S // PART
 S_BANKS = 4
 ACT_BANKS = 3
 E_SLOTS = 6
-ARG_LEAD = 8
+ARG_LEAD = 12
 OUT_SCALE = 1.0 / math.sqrt(S)
 
 
@@ -45,14 +45,16 @@ def tile_irregulartwosidedssdsmoother_x1_kernel(tc, c, b, x, t, dt, lf, lb, out_
             banks_taken.append(tag)
             return ps.tile([PART, KP], F32, name=tag, tag=tag)
 
-        t_sb = sbuf([PART, HALVES, PACK], BF16, "t_sb")
-        dt_sb = sbuf([PART, HALVES, PACK], BF16, "dt_sb")
+        t_sb = sbuf([PART, HALVES, 16], BF16, "t_sb")
+        dt_sb = sbuf([PART, HALVES, 16], BF16, "dt_sb")
         lf_sb = sbuf([PART, B], BF16, "lf_sb")
         lb_sb = sbuf([PART, B], BF16, "lb_sb")
-        nc.sync.dma_start(out=t_sb[:], in_=t.rearrange("n (g p j) -> p (n g) j", g=2, j=PACK))
-        nc.scalar.dma_start(out=dt_sb[:], in_=dt.rearrange("n (g p j) -> p (n g) j", g=2, j=PACK))
+        t_view = t.rearrange("n (g p j) -> p (n g) j", g=2, j=PACK)
+        nc.sync.dma_start(out=t_sb[:, 0:2, 0:PACK], in_=t_view[:, 0:2, :])
+        nc.scalar.dma_start(out=lb_sb[:], in_=lb.partition_broadcast(PART))
         nc.sync.dma_start(out=lf_sb[:], in_=lf.partition_broadcast(PART))
-        nc.sync.dma_start(out=lb_sb[:], in_=lb.partition_broadcast(PART))
+        nc.scalar.dma_start(out=dt_sb[:, :, 0:PACK], in_=dt.rearrange("n (g p j) -> p (n g) j", g=2, j=PACK))
+        nc.sync.dma_start(out=t_sb[:, 2:4, 0:PACK], in_=t_view[:, 2:4, :])
 
         raw = {}
 
@@ -74,22 +76,16 @@ def tile_irregulartwosidedssdsmoother_x1_kernel(tc, c, b, x, t, dt, lf, lb, out_
         ident = sbuf([PART, PART], F32, "ident")
         make_identity(nc, ident[:])
 
-        one = sbuf([PART, 1], F32, "one")
-        warm = sbuf([PART, 1], F32, "warm")
-        nc.vector.memset(one[:], 1.0)
-        nc.scalar.activation(out=warm[:], in_=one[:], func=ACT.Ln)
 
         COLS = HALVES * PACK
         fwd = sbuf([PART, COLS], F32, "fwd")
         bwd = sbuf([PART, COLS], F32, "bwd")
         both = sbuf([PART, COLS], F32, "both")
-        t_flat = t_sb[:].rearrange("p h j -> p (h j)")
         dt32 = sbuf([PART, COLS], F32, "dt32")
         mant = sbuf([PART, COLS], I32, "mant")
         expo_i = sbuf([PART, COLS], I32, "expo_i")
         sign = sbuf([PART, COLS], I32, "sign")
         ln_mant = sbuf([PART, COLS], F32, "ln_mant")
-        warm2 = sbuf([PART, 1], F32, "warm2")
         expo = sbuf([PART, COLS], F32, "expo")
         k1 = sbuf([PART, COLS], F32, "k1")
         k2 = sbuf([PART, COLS], F32, "k2")
@@ -100,13 +96,14 @@ def tile_irregulartwosidedssdsmoother_x1_kernel(tc, c, b, x, t, dt, lf, lb, out_
 
         def rates(n):
             cols = slice(n * 8, n * 8 + 8)
-            nc.vector.tensor_scalar(out=bwd[:, cols], in0=t_flat[:, cols], scalar1=lb_sb[:, n:n + 1],
-                                    scalar2=None, op0=ALU.mult)
-            nc.vector.tensor_scalar(out=fwd[:, cols], in0=t_flat[:, cols], scalar1=lf_sb[:, n:n + 1],
-                                    scalar2=-1.0, op0=ALU.mult, op1=ALU.mult)
+            times = t_sb[:, 2 * n:2 * n + 2, 0:PACK]
+            nc.vector.tensor_scalar(out=bwd[:, cols].rearrange("p (h j) -> p h j", j=PACK), in0=times,
+                                    scalar1=lb_sb[:, n:n + 1], scalar2=None, op0=ALU.mult)
+            nc.vector.tensor_scalar(out=fwd[:, cols].rearrange("p (h j) -> p h j", j=PACK), in0=times,
+                                    scalar1=lf_sb[:, n:n + 1], scalar2=-1.0, op0=ALU.mult, op1=ALU.mult)
 
-        nc.vector.tensor_copy(out=dt32[:], in_=dt_sb[:].rearrange("p h j -> p (h j)"))
         rates(0)
+        nc.vector.tensor_copy(out=dt32[:].rearrange("p (h j) -> p h j", j=PACK), in_=dt_sb[:, :, 0:PACK])
         rates(1)
         nc.vector.tensor_scalar(out=mant[:], in0=bits, scalar1=0x007FFFFF, scalar2=0x3F800000,
                                 op0=ALU.bitwise_and, op1=ALU.bitwise_or)
@@ -116,13 +113,14 @@ def tile_irregulartwosidedssdsmoother_x1_kernel(tc, c, b, x, t, dt, lf, lb, out_
                                 op0=ALU.bitwise_and, op1=ALU.bitwise_or)
         nc.vector.tensor_tensor(out=both[:], in0=bwd[:], in1=fwd[:], op=ALU.subtract)
         nc.scalar.activation(out=ln_mant[:], in_=mant[:].bitcast(F32), func=ACT.Ln)
-        nc.scalar.activation(out=warm2[:], in_=one[:], func=ACT.Exp)
         nc.vector.tensor_copy(out=expo[:], in_=expo_i[:])
-        nc.vector.tensor_tensor(out=k4[:], in0=ln_mant[:], in1=bwd[:], op=ALU.subtract)
-        nc.vector.tensor_scalar(out=k1[:], in0=expo[:], scalar1=-127.0, scalar2=math.log(2.0),
-                                op0=ALU.add, op1=ALU.mult)
-        nc.vector.tensor_scalar(out=k2[:], in0=expo[:], scalar1=0.0, scalar2=-1e30,
-                                op0=ALU.is_equal, op1=ALU.mult)
+
+        def bias_a():
+            nc.vector.tensor_scalar(out=k1[:], in0=expo[:], scalar1=-127.0, scalar2=math.log(2.0),
+                                    op0=ALU.add, op1=ALU.mult)
+            nc.vector.tensor_scalar(out=k2[:], in0=expo[:], scalar1=0.0, scalar2=-1e30,
+                                    op0=ALU.is_equal, op1=ALU.mult)
+            nc.vector.tensor_tensor(out=k4[:], in0=ln_mant[:], in1=bwd[:], op=ALU.subtract)
 
         def bias_b():
             nc.vector.tensor_tensor(out=k3[:], in0=k1[:], in1=k2[:], op=ALU.add)
@@ -187,21 +185,19 @@ def tile_irregulartwosidedssdsmoother_x1_kernel(tc, c, b, x, t, dt, lf, lb, out_
                                in_=bank[:].rearrange("p (r u m) -> p r m u", r=2, u=2))
 
 
-        def sign_x(h, j):
-            col = h * PACK + j
-            nc.vector.tensor_scalar(out=raw["x", h][:, j, :], in0=raw["x", h][:, j, :],
-                                    scalar1=sign[:].bitcast(F32)[:, col:col + 1], scalar2=None, op0=ALU.mult)
-
-        def interleave_x(h, half, eng):
+        def regroup_x(h, half):
             if half == 0:
                 new_grouped(("x", h))
-            dst = grouped["x", h][:].rearrange("p (s c m j) -> p c s m j", s=PACK, m=2, j=PACK)
-            src = raw["x", h][:].rearrange("p j (c m s) -> p c s m j", s=PACK, m=2)
-            cs = slice(half * 32, half * 32 + 32)
-            if eng == "v":
-                nc.vector.tensor_copy(out=dst[:, cs], in_=src[:, cs])
-            else:
-                nc.scalar.copy(out=dst[:, cs], in_=src[:, cs])
+            cols = slice(half * 256, half * 256 + 256)
+            for j in range(PACK):
+                col = h * PACK + j
+                nc.vector.tensor_scalar(out=raw["x", h][:, j, cols], in0=raw["x", h][:, j, cols],
+                                        scalar1=sign[:].bitcast(F32)[:, col:col + 1], scalar2=None, op0=ALU.mult)
+            dst = grouped["x", h][:].rearrange("p (s m j) -> p s m j", s=PACK, j=PACK)
+            src = raw["x", h][:].rearrange("p j (m s) -> p s m j", s=PACK)
+            ms = slice(half * 64, half * 64 + 64)
+            nc.gpsimd.tensor_scalar(out=dst[:, :, ms, :], in0=src[:, :, ms, :], scalar1=1.0, scalar2=0.0,
+                                    op0=ALU.mult, op1=ALU.add)
 
         def quantize(which, h):
             codes[which, h] = sbuf([PART, KP], U32, "codes_%s%d" % (which, h))
@@ -327,18 +323,20 @@ def tile_irregulartwosidedssdsmoother_x1_kernel(tc, c, b, x, t, dt, lf, lb, out_
 
         spread_bwd(0)
         spread_fwd(0)
-        bias_b()
         copy_bwd(0, "v")
-        bias_c()
+        bias_a()
         turn("b", 0, 0)
         turn("b", 0, 1)
+        bias_b()
         arg(0)
+        bias_c()
         arg(1)
+        expo_step(0)
         copy_turned("b", 0, 0)
         turn("c", 0, 0)
-        expo_step(0)
         copy_turned("b", 0, 1)
         turn("c", 0, 1)
+        regroup_x(0, 0)
         arg(2)
         expo_step(1)
         arg(3)
@@ -348,45 +346,42 @@ def tile_irregulartwosidedssdsmoother_x1_kernel(tc, c, b, x, t, dt, lf, lb, out_
         copy_turned("c", 0, 1)
         spread_bwd(1)
         quantize("b", 0)
+        regroup_x(0, 1)
         arg(5)
-        expo_step(2)
         copy_turned("b", 1, 0)
-        turn("b", 1, 1)
         arg(6)
-        expo_step(3)
-        arg(7)
-        copy_turned("b", 1, 1)
-        spread_fwd(1)
-        quantize("c", 0)
         copy_bwd(1, "a")
-        turn("c", 1, 0)
-        for j in range(PACK):
-            sign_x(0, j)
-        for j in range(PACK):
-            sign_x(1, j)
+        arg(7)
+        expo_step(2)
+        spread_fwd(1)
+        turn("b", 1, 1)
+        quantize("c", 0)
+        regroup_x(1, 0)
+        expo_step(3)
         expo_step(4)
+        copy_turned("b", 1, 1)
         expo_step(5)
         scores(0, 0)
-        interleave_x(0, 0, "v")
-        interleave_x(0, 1, "v")
+        turn("c", 1, 0)
+        arg(8)
+        arg(9)
+        arg(10)
         quantize("b", 1)
         expo_step(6)
         expo_step(7)
         scores(0, 1)
-        interleave_x(1, 0, "v")
         quantize("x", 0)
-        interleave_x(1, 1, "v")
+        regroup_x(1, 1)
         copy_turned("c", 1, 0)
-        for a in range(8, ARG_LEAD):
-            arg(a)
+        arg(11)
 
         turns = {0: [("c", 1, 1), ("b", 2, 0)], 1: [("b", 2, 1)], 2: [("b", 3, 0)], 3: [("b", 3, 1)],
-                 4: [("c", 2, 0)], 5: [("c", 2, 1)], 8: [("c", 3, 0)], 9: [("c", 3, 1)]}
-        quants = {0: ("x", 1), 1: ("c", 1), 2: ("b", 2), 4: ("b", 3), 6: ("c", 2), 7: ("x", 2), 8: ("x", 3), 10: ("c", 3)}
-        signs = {3: 2, 5: 3}
-        x_copies = {4: (2, 0), 5: (2, 1), 6: (3, 0), 7: (3, 1)}
-        arg_counts = [2, 3, 3, 2, 2, 2, 2, 2, 2, 2, 2, 0, 0, 0, 0, 0]
-        y_quant = {11: (0, 4), 12: (4, 8), 13: (8, 12), 15: (12, 14)}
+                 4: [("c", 2, 0)], 5: [("c", 2, 1)], 7: [("c", 3, 0)], 8: [("c", 3, 1)]}
+        quants = {0: ("x", 1), 1: ("c", 1), 2: ("b", 2), 4: ("b", 3), 5: ("x", 2), 6: ("c", 2), 7: ("x", 3), 9: ("c", 3)}
+        regroups = {2: (2, 0), 3: (2, 1), 4: (3, 0), 5: (3, 1)}
+        arg_counts = [1, 1, 2, 2, 2, 2, 2, 2, 2, 1, 2, 1, 0, 0, 0, 0]
+        y_quant = {11: (0, 4), 12: (4, 8), 13: (8, 12), 14: (12, 13), 15: (13, 14)}
+        y_stores = {11: (0, 4), 12: (4, 8), 13: (8, 12), 15: (12, 14)}
         next_arg = ARG_LEAD
         next_exp = 8
         last = UNITS - 1
@@ -397,8 +392,7 @@ def tile_irregulartwosidedssdsmoother_x1_kernel(tc, c, b, x, t, dt, lf, lb, out_
                     next_exp += 1
             todo = list(range(next_arg, next_arg + arg_counts[u]))
             next_arg += arg_counts[u]
-            new_half = next_arg % 8 == 0 and next_arg < 8 * HALVES and todo
-            if todo and todo[0] % 8 == 0 and todo[0] > 8:
+            if todo and todo[0] % 8 == 0:
                 spread_fwd(todo[0] // 8)
             if u < last:
                 scores(u + 1, 0)
@@ -414,24 +408,20 @@ def tile_irregulartwosidedssdsmoother_x1_kernel(tc, c, b, x, t, dt, lf, lb, out_
             for job in turns.get(u, []):
                 turn(*job)
                 copy_turned(*job)
-            if new_half:
-                spread_bwd(next_arg // 8)
-                copy_bwd(next_arg // 8, "a")
-            if todo:
-                arg(todo[0])
-            if u in signs:
-                for j in range(PACK):
-                    sign_x(signs[u], j)
+            if u in (1, 5):
+                spread_bwd(u // 4 + 2)
+                copy_bwd(u // 4 + 2, "a")
+            for a in todo:
+                arg(a)
             if u in y_quant:
                 quantize_y(*y_quant[u])
-                store_words(*y_quant[u])
+                if u in y_stores:
+                    store_words(*y_stores[u])
             quantize_m(u)
-            for a in todo[1:]:
-                arg(a)
             if u in quants:
                 quantize(*quants[u])
-            if u in x_copies:
-                interleave_x(*x_copies[u], "a")
+            if u in regroups:
+                regroup_x(*regroups[u])
             if u == 13:
                 store_scales(0, 12, [nc.sync])
         out_cols(last)

@@ -24,7 +24,7 @@ UNITS = B * S // PART
 S_BANKS = 4
 ACT_BANKS = 3
 E_SLOTS = 6
-ARG_LEAD = 12
+ARG_LEAD = 14
 OUT_SCALE = 1.0 / math.sqrt(S)
 
 
@@ -137,7 +137,8 @@ def tile_irregulartwosidedssdsmoother_x1_kernel(tc, c, b, x, t, dt, lf, lb, out_
                                     col_tile[:, col:col + 1].to_broadcast([PART, PART]), ident[:])
 
         def spread_fwd(h):
-            fwd_row[h] = ps.tile([PART, KP], F32, name="fwd_row", tag="fwd_row")
+            tag = "s%d" % (S_BANKS - 1) if h == 0 else "fwd_row"
+            fwd_row[h] = ps.tile([PART, KP], F32, name=tag, tag=tag)
             spread(fwd_row[h], fwd, h)
 
         def spread_bwd(h):
@@ -286,15 +287,12 @@ def tile_irregulartwosidedssdsmoother_x1_kernel(tc, c, b, x, t, dt, lf, lb, out_
 
         out_flat = out_0.rearrange("n i w -> (n i) w")
 
-        def store_rows(u, eng):
+        def store_rows(u, queue):
             y = sbuf([PART, P], F32, "y%d" % (u % 6))
             dst = y[:].rearrange("p (m s) -> p m s", s=PACK)
             src = row_bank[u][:].rearrange("p (s m) -> p m s", s=PACK)
-            if eng == "v":
-                nc.vector.tensor_scalar(out=dst, in0=src, scalar1=OUT_SCALE, scalar2=None, op0=ALU.mult)
-            else:
-                nc.scalar.activation(out=dst, in_=src, func=ACT.Copy, scale=OUT_SCALE)
-            nc.sync.dma_start(out=out_flat[u * PART:(u + 1) * PART, :], in_=y[:])
+            nc.scalar.activation(out=dst, in_=src, func=ACT.Copy, scale=OUT_SCALE)
+            queue.dma_start(out=out_flat[u * PART:(u + 1) * PART, :], in_=y[:])
 
         y_bf = sbuf([PART, B * S * PACK], BF16, "y_bf")
 
@@ -323,7 +321,9 @@ def tile_irregulartwosidedssdsmoother_x1_kernel(tc, c, b, x, t, dt, lf, lb, out_
 
         spread_bwd(0)
         spread_fwd(0)
-        copy_bwd(0, "v")
+        spread_bwd(1)
+        spread_fwd(1)
+        copy_bwd(0, "a")
         bias_a()
         turn("b", 0, 0)
         turn("b", 0, 1)
@@ -332,56 +332,51 @@ def tile_irregulartwosidedssdsmoother_x1_kernel(tc, c, b, x, t, dt, lf, lb, out_
         bias_c()
         arg(1)
         expo_step(0)
-        copy_turned("b", 0, 0)
-        turn("c", 0, 0)
-        copy_turned("b", 0, 1)
-        turn("c", 0, 1)
-        regroup_x(0, 0)
-        arg(2)
-        expo_step(1)
-        arg(3)
-        copy_turned("c", 0, 0)
-        turn("b", 1, 0)
-        arg(4)
-        copy_turned("c", 0, 1)
-        spread_bwd(1)
-        quantize("b", 0)
-        regroup_x(0, 1)
-        arg(5)
-        copy_turned("b", 1, 0)
-        arg(6)
         copy_bwd(1, "a")
-        arg(7)
+        turn("c", 0, 0)
+        regroup_x(0, 0)
+        for a in range(2, 6):
+            arg(a)
+        copy_turned("b", 0, 0)
+        turn("c", 0, 1)
+        expo_step(1)
+        copy_turned("b", 0, 1)
+        turn("b", 1, 0)
         expo_step(2)
-        spread_fwd(1)
+        regroup_x(0, 1)
+        for a in range(6, 10):
+            arg(a)
+        copy_turned("c", 0, 0)
         turn("b", 1, 1)
-        quantize("c", 0)
-        regroup_x(1, 0)
         expo_step(3)
-        expo_step(4)
-        copy_turned("b", 1, 1)
-        expo_step(5)
-        scores(0, 0)
+        copy_turned("c", 0, 1)
         turn("c", 1, 0)
-        arg(8)
-        arg(9)
-        arg(10)
-        quantize("b", 1)
+        expo_step(4)
+        quantize("b", 0)
+        regroup_x(1, 0)
+        for a in range(10, ARG_LEAD):
+            arg(a)
+        copy_turned("b", 1, 0)
+        turn("c", 1, 1)
+        expo_step(5)
+        copy_turned("b", 1, 1)
         expo_step(6)
         expo_step(7)
+        quantize("c", 0)
+        scores(0, 0)
+        quantize("b", 1)
         scores(0, 1)
         quantize("x", 0)
         regroup_x(1, 1)
         copy_turned("c", 1, 0)
-        arg(11)
+        copy_turned("c", 1, 1)
 
-        turns = {0: [("c", 1, 1), ("b", 2, 0)], 1: [("b", 2, 1)], 2: [("b", 3, 0)], 3: [("b", 3, 1)],
+        turns = {0: [("b", 2, 0), ("b", 2, 1)], 2: [("b", 3, 0)], 3: [("b", 3, 1)],
                  4: [("c", 2, 0)], 5: [("c", 2, 1)], 7: [("c", 3, 0)], 8: [("c", 3, 1)]}
         quants = {0: ("x", 1), 1: ("c", 1), 2: ("b", 2), 4: ("b", 3), 5: ("x", 2), 6: ("c", 2), 7: ("x", 3), 9: ("c", 3)}
-        regroups = {2: (2, 0), 3: (2, 1), 4: (3, 0), 5: (3, 1)}
-        arg_counts = [1, 1, 2, 2, 2, 2, 2, 2, 2, 1, 2, 1, 0, 0, 0, 0]
+        regroups = {1: (2, 0), 2: (2, 1), 3: (3, 0), 4: (3, 1)}
+        arg_counts = [2, 0, 2, 2, 2, 2, 0, 2, 2, 2, 2, 0, 0, 0, 0, 0]
         y_quant = {11: (0, 4), 12: (4, 8), 13: (8, 12), 14: (12, 13), 15: (13, 14)}
-        y_stores = {11: (0, 4), 12: (4, 8), 13: (8, 12), 15: (12, 14)}
         next_arg = ARG_LEAD
         next_exp = 8
         last = UNITS - 1
@@ -392,15 +387,17 @@ def tile_irregulartwosidedssdsmoother_x1_kernel(tc, c, b, x, t, dt, lf, lb, out_
                     next_exp += 1
             todo = list(range(next_arg, next_arg + arg_counts[u]))
             next_arg += arg_counts[u]
-            if todo and todo[0] % 8 == 0:
-                spread_fwd(todo[0] // 8)
+            if u in (1, 6):
+                spread_bwd(next_arg // 8)
+                spread_fwd(next_arg // 8)
+                copy_bwd(next_arg // 8, "a")
             if u < last:
                 scores(u + 1, 0)
                 scores(u + 1, 1)
             if u >= 1:
                 out_rows(u - 1)
                 out_cols(u - 1)
-                store_rows(u - 1, "a")
+                store_rows(u - 1, nc.sync)
             weigh(u, 0)
             weigh(u, 1)
             if u >= 1:
@@ -408,17 +405,15 @@ def tile_irregulartwosidedssdsmoother_x1_kernel(tc, c, b, x, t, dt, lf, lb, out_
             for job in turns.get(u, []):
                 turn(*job)
                 copy_turned(*job)
-            if u in (1, 5):
-                spread_bwd(u // 4 + 2)
-                copy_bwd(u // 4 + 2, "a")
             for a in todo:
                 arg(a)
             if u in y_quant:
                 quantize_y(*y_quant[u])
-                if u in y_stores:
-                    store_words(*y_stores[u])
+                store_words(*y_quant[u])
+            if u in quants and not todo:
+                quantize(*quants[u])
             quantize_m(u)
-            if u in quants:
+            if u in quants and todo:
                 quantize(*quants[u])
             if u in regroups:
                 regroup_x(*regroups[u])
@@ -427,8 +422,9 @@ def tile_irregulartwosidedssdsmoother_x1_kernel(tc, c, b, x, t, dt, lf, lb, out_
         out_cols(last)
         out_rows(last)
         quantize_y(last - 1, last)
+        store_words(last - 1, last)
         copy_cols(last)
-        store_rows(last, "a")
+        store_rows(last, nc.scalar)
         quantize_y(last, UNITS)
-        store_words(last - 1, UNITS)
-        store_scales(12, UNITS, [nc.scalar, nc.sync])
+        store_words(last, UNITS)
+        store_scales(12, UNITS, [nc.sync, nc.scalar])

import math
from contextlib import ExitStack

import concourse.mybir as mybir
from concourse.masks import make_identity

B, S, N, P = 2, 1024, 512, 512
FLOPS = 2 * B * S * S * N + 2 * B * S * S * P

F32 = mybir.dt.float32
BF16 = mybir.dt.bfloat16
I32 = mybir.dt.int32
U32 = mybir.dt.uint32
U8 = mybir.dt.uint8
FP8X4 = mybir.dt.float8_e4m3fn_x4
ALU = mybir.AluOpType
ACT = mybir.ActivationFunctionType

PART = 128
PACK = 4
KP = PART * PACK
HALVES = B * S // KP
UNITS = B * S // PART
S_BANKS = 4
ACT_BANKS = 3
E_SLOTS = 6
ARG_LEAD = 14
OUT_SCALE = 1.0 / math.sqrt(S)


def tile_irregulartwosidedssdsmoother_x1_kernel(tc, c, b, x, t, dt, lf, lb, out_0, out_1, out_2):
    nc = tc.nc
    with ExitStack() as ctx:
        sb = ctx.enter_context(tc.tile_pool(name="sb", bufs=1))
        ps = ctx.enter_context(tc.psum_pool(name="ps", bufs=1))
        ctx.enter_context(tc.manual_schedule())

        def sbuf(shape, dtype, tag):
            return sb.tile(shape, dtype, name=tag, tag=tag, align_bytes=64)

        banks_taken = []

        def act_bank():
            tag = "act%d" % (len(banks_taken) % ACT_BANKS)
            banks_taken.append(tag)
            return ps.tile([PART, KP], F32, name=tag, tag=tag)

        t_sb = sbuf([PART, HALVES, 16], BF16, "t_sb")
        dt_sb = sbuf([PART, HALVES, 16], BF16, "dt_sb")
        lf_sb = sbuf([PART, B], BF16, "lf_sb")
        lb_sb = sbuf([PART, B], BF16, "lb_sb")
        t_view = t.rearrange("n (g p j) -> p (n g) j", g=2, j=PACK)
        nc.sync.dma_start(out=t_sb[:, 0:2, 0:PACK], in_=t_view[:, 0:2, :])
        nc.scalar.dma_start(out=lb_sb[:], in_=lb.partition_broadcast(PART))
        nc.sync.dma_start(out=lf_sb[:], in_=lf.partition_broadcast(PART))
        nc.scalar.dma_start(out=dt_sb[:, :, 0:PACK], in_=dt.rearrange("n (g p j) -> p (n g) j", g=2, j=PACK))
        nc.sync.dma_start(out=t_sb[:, 2:4, 0:PACK], in_=t_view[:, 2:4, :])

        raw = {}

        def load(which, h):
            n, g = divmod(h, 2)
            rows = {"b": b, "c": c, "x": x}[which][n, g * KP:(g + 1) * KP, :]
            raw[which, h] = sbuf([PART, PACK, N], BF16, "raw_%s%d" % (which, h))
            if which == "c":
                nc.sync.dma_start(
                    out=raw[which, h][:].rearrange("p (q r) k -> p q (r k)", r=2),
                    in_=rows.rearrange("(q p r) k -> p q (r k)", q=2, r=2))
            else:
                nc.sync.dma_start(out=raw[which, h][:], in_=rows.rearrange("(p j) k -> p j k", j=PACK))

        for which, h in [("b", 0), ("x", 0), ("c", 0), ("b", 1), ("x", 1), ("c", 1),
                         ("b", 2), ("b", 3), ("x", 2), ("c", 2), ("x", 3), ("c", 3)]:
            load(which, h)

        ident = sbuf([PART, PART], F32, "ident")
        make_identity(nc, ident[:])


        COLS = HALVES * PACK
        fwd = sbuf([PART, COLS], F32, "fwd")
        bwd = sbuf([PART, COLS], F32, "bwd")
        both = sbuf([PART, COLS], F32, "both")
        dt32 = sbuf([PART, COLS], F32, "dt32")
        mant = sbuf([PART, COLS], I32, "mant")
        expo_i = sbuf([PART, COLS], I32, "expo_i")
        sign = sbuf([PART, COLS], I32, "sign")
        ln_mant = sbuf([PART, COLS], F32, "ln_mant")
        expo = sbuf([PART, COLS], F32, "expo")
        k1 = sbuf([PART, COLS], F32, "k1")
        k2 = sbuf([PART, COLS], F32, "k2")
        k3 = sbuf([PART, COLS], F32, "k3")
        k4 = sbuf([PART, COLS], F32, "k4")
        bias = sbuf([PART, COLS], F32, "bias")
        bits = dt32[:].bitcast(I32)

        def rates(n):
            cols = slice(n * 8, n * 8 + 8)
            times = t_sb[:, 2 * n:2 * n + 2, 0:PACK]
            nc.vector.tensor_scalar(out=bwd[:, cols].rearrange("p (h j) -> p h j", j=PACK), in0=times,
                                    scalar1=lb_sb[:, n:n + 1], scalar2=None, op0=ALU.mult)
            nc.vector.tensor_scalar(out=fwd[:, cols].rearrange("p (h j) -> p h j", j=PACK), in0=times,
                                    scalar1=lf_sb[:, n:n + 1], scalar2=-1.0, op0=ALU.mult, op1=ALU.mult)

        rates(0)
        nc.vector.tensor_copy(out=dt32[:].rearrange("p (h j) -> p h j", j=PACK), in_=dt_sb[:, :, 0:PACK])
        rates(1)
        nc.vector.tensor_scalar(out=mant[:], in0=bits, scalar1=0x007FFFFF, scalar2=0x3F800000,
                                op0=ALU.bitwise_and, op1=ALU.bitwise_or)
        nc.vector.tensor_scalar(out=expo_i[:], in0=bits, scalar1=23, scalar2=0xFF,
                                op0=ALU.logical_shift_right, op1=ALU.bitwise_and)
        nc.vector.tensor_scalar(out=sign[:], in0=bits, scalar1=-0x80000000, scalar2=0x3F800000,
                                op0=ALU.bitwise_and, op1=ALU.bitwise_or)
        nc.vector.tensor_tensor(out=both[:], in0=bwd[:], in1=fwd[:], op=ALU.subtract)
        nc.scalar.activation(out=ln_mant[:], in_=mant[:].bitcast(F32), func=ACT.Ln)
        nc.vector.tensor_copy(out=expo[:], in_=expo_i[:])

        def bias_a():
            nc.vector.tensor_scalar(out=k1[:], in0=expo[:], scalar1=-127.0, scalar2=math.log(2.0),
                                    op0=ALU.add, op1=ALU.mult)
            nc.vector.tensor_scalar(out=k2[:], in0=expo[:], scalar1=0.0, scalar2=-1e30,
                                    op0=ALU.is_equal, op1=ALU.mult)
            nc.vector.tensor_tensor(out=k4[:], in0=ln_mant[:], in1=bwd[:], op=ALU.subtract)

        def bias_b():
            nc.vector.tensor_tensor(out=k3[:], in0=k1[:], in1=k2[:], op=ALU.add)

        def bias_c():
            nc.vector.tensor_tensor(out=bias[:], in0=k3[:], in1=k4[:], op=ALU.add)

        fwd_row, bwd_bank, bwd_row = {}, {}, {}

        def spread(bank, col_tile, h):
            for j in range(PACK):
                col = h * PACK + j
                nc.tensor.transpose(bank[:, j * PART:(j + 1) * PART],
                                    col_tile[:, col:col + 1].to_broadcast([PART, PART]), ident[:])

        def spread_fwd(h):
            tag = "s%d" % (S_BANKS - 1) if h == 0 else "fwd_row"
            fwd_row[h] = ps.tile([PART, KP], F32, name=tag, tag=tag)
            spread(fwd_row[h], fwd, h)

        def spread_bwd(h):
            bwd_bank[h] = act_bank()
            spread(bwd_bank[h], bwd, h)

        def copy_bwd(h, eng):
            bwd_row[h] = sbuf([PART, KP], F32, "bwd_row%d" % h)
            src = bwd_bank[h][:].rearrange("p (j m) -> p m j", j=PACK)
            dst = bwd_row[h][:].rearrange("p (m j) -> p m j", j=PACK)
            if eng == "v":
                nc.vector.tensor_copy(out=dst, in_=src)
            else:
                nc.scalar.copy(out=dst, in_=src)

        turned, grouped, codes, scales = {}, {}, {}, {}

        def new_grouped(key):
            if key[0] == "x":
                tag = "grouped_x%d" % key[1]
            else:
                tag = "grouped%d" % (len([q for q in grouped if q[0] != "x"]) % 3)
            grouped[key] = sbuf([PART, KP * PACK], BF16, tag)

        def turn(which, h, q):
            words = raw[which, h][:].rearrange("p s k -> p (s k)").bitcast(F32)
            bank = act_bank()
            turned[which, h, q] = bank
            for r in range(2):
                for u in range(2):
                    w0 = (2 * q + r) * 256 + u
                    nc.tensor.transpose(bank[:, (2 * r + u) * PART:(2 * r + u + 1) * PART],
                                        words[:, w0:(2 * q + r + 1) * 256:2], ident[:])

        def copy_turned(which, h, q):
            if q == 0:
                new_grouped((which, h))
            dst = grouped[which, h][:, q * 1024:(q + 1) * 1024].bitcast(F32)
            bank = turned[which, h, q]
            if which == "c":
                nc.scalar.copy(out=dst.rearrange("p (m r u) -> p m r u", r=2, u=2),
                               in_=bank[:].rearrange("p (r u m) -> p m r u", r=2, u=2))
            else:
                nc.scalar.copy(out=dst.rearrange("p (r m u) -> p r m u", r=2, u=2),
                               in_=bank[:].rearrange("p (r u m) -> p r m u", r=2, u=2))


        def regroup_x(h, half):
            if half == 0:
                new_grouped(("x", h))
            cols = slice(half * 256, half * 256 + 256)
            for j in range(PACK):
                col = h * PACK + j
                nc.vector.tensor_scalar(out=raw["x", h][:, j, cols], in0=raw["x", h][:, j, cols],
                                        scalar1=sign[:].bitcast(F32)[:, col:col + 1], scalar2=None, op0=ALU.mult)
            dst = grouped["x", h][:].rearrange("p (s m j) -> p s m j", s=PACK, j=PACK)
            src = raw["x", h][:].rearrange("p j (m s) -> p s m j", s=PACK)
            ms = slice(half * 64, half * 64 + 64)
            nc.gpsimd.tensor_scalar(out=dst[:, :, ms, :], in0=src[:, :, ms, :], scalar1=1.0, scalar2=0.0,
                                    op0=ALU.mult, op1=ALU.add)

        def quantize(which, h):
            codes[which, h] = sbuf([PART, KP], U32, "codes_%s%d" % (which, h))
            scales[which, h] = sbuf([PART, KP], U8, "scales_%s%d" % (which, h))
            nc.vector.quantize_mx(out=codes[which, h][:].bitcast(FP8X4), scales=scales[which, h][:],
                                  in_=grouped[which, h][:])

        decay = {}

        def arg(a):
            h, rest = divmod(a, 8)
            g, j = divmod(rest, PACK)
            if j == 0:
                decay[h, g] = sbuf([PART, PACK, KP], F32, "decay%d" % ((2 * h + g) % E_SLOTS))
            col = ((h // 2) * 2 + g) * PACK + j
            nc.vector.scalar_tensor_tensor(
                out=decay[h, g][:, j, :].rearrange("p (m r) -> p m r", r=PACK),
                in0=fwd_row[h][:].rearrange("p (r m) -> p m r", r=PACK),
                scalar=both[:, col:col + 1],
                in1=bwd_row[h][:].rearrange("p (m r) -> p m r", r=PACK),
                op0=ALU.add, op1=ALU.min)

        def expo_step(a):
            h, rest = divmod(a, 8)
            g, j = divmod(rest, PACK)
            col = ((h // 2) * 2 + g) * PACK + j
            nc.scalar.activation(out=decay[h, g][:, j, :], in_=decay[h, g][:, j, :], func=ACT.Exp,
                                 bias=bias[:, col:col + 1])

        s_bank, m_bf, m_codes, m_scales = {}, {}, {}, {}

        def scores(u, g):
            h, ib = divmod(u, PACK)
            hb = (h // 2) * 2 + g
            tag = "s%d" % ((2 * u + g) % S_BANKS)
            s_bank[u, g] = ps.tile([PART, KP], F32, name=tag, tag=tag)
            cols = slice(ib * PART, (ib + 1) * PART)
            for j in range(PACK):
                js = slice(j * PART, (j + 1) * PART)
                nc.tensor.matmul_mx(out=s_bank[u, g][:, js],
                                    lhsT=codes["b", hb][:, js].bitcast(FP8X4), lhsT_scale=scales["b", hb][:, js],
                                    rhs=codes["c", h][:, cols].bitcast(FP8X4), rhs_scale=scales["c", h][:, cols],
                                    start=True, stop=True)

        def weigh(u, g):
            h, ib = divmod(u, PACK)
            if g == 0:
                m_bf[u] = sbuf([PART, 2 * KP], BF16, "m_bf%d" % (u % 4))
            nc.vector.tensor_tensor(
                out=m_bf[u][:, g * KP:(g + 1) * KP].rearrange("p (c i j) -> p c j i", i=2, j=PACK),
                in0=s_bank[u, g][:].rearrange("p (j c i) -> p c j i", j=PACK, i=2),
                in1=decay[h, g][:, :, ib * PART:(ib + 1) * PART].rearrange("p j (c i) -> p c j i", i=2),
                op=ALU.mult)

        def quantize_m(u):
            m_codes[u] = sbuf([PART, 2 * PART], U32, "m_codes%d" % (u % 4))
            m_scales[u] = sbuf([PART, 2 * PART], U8, "m_scales%d" % (u % 4))
            nc.vector.quantize_mx(out=m_codes[u][:].bitcast(FP8X4), scales=m_scales[u][:], in_=m_bf[u][:])

        row_bank, col_bank = {}, {}
        y_codes = sbuf([PART, B * S], U32, "y_codes")
        y_scales = sbuf([PART, B * S], U8, "y_scales")

        def out_rows(u):
            n = u // 8
            row_bank[u] = act_bank()
            for g in range(2):
                ms = slice(g * PART, (g + 1) * PART)
                nc.tensor.matmul_mx(out=row_bank[u][:],
                                    lhsT=m_codes[u][:, ms].bitcast(FP8X4), lhsT_scale=m_scales[u][:, ms],
                                    rhs=codes["x", 2 * n + g][:].bitcast(FP8X4), rhs_scale=scales["x", 2 * n + g][:],
                                    start=(g == 0), stop=(g == 1))

        def out_cols(u):
            n = u // 8
            col_bank[u] = act_bank()
            for s in range(PACK):
                cs = slice(s * PART, (s + 1) * PART)
                for g in range(2):
                    ms = slice(g * PART, (g + 1) * PART)
                    nc.tensor.matmul_mx(out=col_bank[u][:, cs],
                                        lhsT=codes["x", 2 * n + g][:, cs].bitcast(FP8X4),
                                        lhsT_scale=scales["x", 2 * n + g][:, cs],
                                        rhs=m_codes[u][:, ms].bitcast(FP8X4), rhs_scale=m_scales[u][:, ms],
                                        start=(g == 0), stop=(g == 1))

        out_flat = out_0.rearrange("n i w -> (n i) w")

        def store_rows(u, queue):
            y = sbuf([PART, P], F32, "y%d" % (u % 6))
            dst = y[:].rearrange("p (m s) -> p m s", s=PACK)
            src = row_bank[u][:].rearrange("p (s m) -> p m s", s=PACK)
            nc.scalar.activation(out=dst, in_=src, func=ACT.Copy, scale=OUT_SCALE)
            queue.dma_start(out=out_flat[u * PART:(u + 1) * PART, :], in_=y[:])

        y_bf = sbuf([PART, B * S * PACK], BF16, "y_bf")

        def copy_cols(u):
            nc.scalar.activation(out=y_bf[:, u * KP:(u + 1) * KP].rearrange("p (i s) -> p i s", s=PACK),
                                 in_=col_bank[u][:].rearrange("p (s i) -> p i s", s=PACK),
                                 func=ACT.Copy, scale=OUT_SCALE)

        def quantize_y(u0, u1):
            cols = slice(u0 * PART, u1 * PART)
            nc.vector.quantize_mx(out=y_codes[:, cols].bitcast(FP8X4), scales=y_scales[:, cols],
                                  in_=y_bf[:, u0 * KP:u1 * KP])

        words_out = out_1.rearrange("g p m t -> p (g m t)").bitcast(I32)
        scales_out = out_2.rearrange("g q m -> (g q) m").bitcast(I32)

        def store_words(u0, u1):
            cols = slice(u0 * PART, u1 * PART)
            nc.sync.dma_start(out=words_out[:, cols], in_=y_codes[:, cols].bitcast(I32))

        def store_scales(u0, u1, engines):
            cols = slice(u0 * 32, u1 * 32)
            for q in range(4):
                engines[q % len(engines)].dma_start(out=scales_out[4 * q:4 * q + 4, cols],
                                                    in_=y_scales[:].bitcast(I32)[32 * q:32 * q + 4, cols])

        spread_bwd(0)
        spread_fwd(0)
        spread_bwd(1)
        spread_fwd(1)
        copy_bwd(0, "a")
        bias_a()
        turn("b", 0, 0)
        turn("b", 0, 1)
        bias_b()
        arg(0)
        bias_c()
        arg(1)
        expo_step(0)
        copy_bwd(1, "a")
        turn("c", 0, 0)
        regroup_x(0, 0)
        for a in range(2, 6):
            arg(a)
        copy_turned("b", 0, 0)
        turn("c", 0, 1)
        expo_step(1)
        copy_turned("b", 0, 1)
        turn("b", 1, 0)
        expo_step(2)
        regroup_x(0, 1)
        for a in range(6, 10):
            arg(a)
        copy_turned("c", 0, 0)
        turn("b", 1, 1)
        expo_step(3)
        copy_turned("c", 0, 1)
        turn("c", 1, 0)
        expo_step(4)
        quantize("b", 0)
        regroup_x(1, 0)
        for a in range(10, ARG_LEAD):
            arg(a)
        copy_turned("b", 1, 0)
        turn("c", 1, 1)
        expo_step(5)
        copy_turned("b", 1, 1)
        expo_step(6)
        expo_step(7)
        quantize("c", 0)
        scores(0, 0)
        quantize("b", 1)
        scores(0, 1)
        quantize("x", 0)
        regroup_x(1, 1)
        copy_turned("c", 1, 0)
        copy_turned("c", 1, 1)

        turns = {0: [("b", 2, 0), ("b", 2, 1)], 2: [("b", 3, 0)], 3: [("b", 3, 1)],
                 4: [("c", 2, 0)], 5: [("c", 2, 1)], 7: [("c", 3, 0)], 8: [("c", 3, 1)]}
        quants = {0: ("x", 1), 1: ("c", 1), 2: ("b", 2), 4: ("b", 3), 5: ("x", 2), 6: ("c", 2), 7: ("x", 3), 9: ("c", 3)}
        regroups = {1: (2, 0), 2: (2, 1), 3: (3, 0), 4: (3, 1)}
        arg_counts = [2, 0, 2, 2, 2, 2, 0, 2, 2, 2, 2, 0, 0, 0, 0, 0]
        y_quant = {11: (0, 4), 12: (4, 8), 13: (8, 12), 14: (12, 13), 15: (13, 14)}
        next_arg = ARG_LEAD
        next_exp = 8
        last = UNITS - 1
        for u in range(UNITS):
            for k in range(3):
                if next_exp < next_arg:
                    expo_step(next_exp)
                    next_exp += 1
            todo = list(range(next_arg, next_arg + arg_counts[u]))
            next_arg += arg_counts[u]
            if u in (1, 6):
                spread_bwd(next_arg // 8)
                spread_fwd(next_arg // 8)
                copy_bwd(next_arg // 8, "a")
            if u < last:
                scores(u + 1, 0)
                scores(u + 1, 1)
            if u >= 1:
                out_rows(u - 1)
                out_cols(u - 1)
                store_rows(u - 1, nc.sync)
            weigh(u, 0)
            weigh(u, 1)
            if u >= 1:
                copy_cols(u - 1)
            for job in turns.get(u, []):
                turn(*job)
                copy_turned(*job)
            for a in todo:
                arg(a)
            if u in y_quant:
                quantize_y(*y_quant[u])
                store_words(*y_quant[u])
            if u in quants and not todo:
                quantize(*quants[u])
            quantize_m(u)
            if u in quants and todo:
                quantize(*quants[u])
            if u in regroups:
                regroup_x(*regroups[u])
            if u == 13:
                store_scales(0, 12, [nc.sync])
        out_cols(last)
        out_rows(last)
        quantize_y(last - 1, last)
        store_words(last - 1, last)
        copy_cols(last)
        store_rows(last, nc.scalar)
        quantize_y(last, UNITS)
        store_words(last, UNITS)
        store_scales(12, UNITS, [nc.sync, nc.scalar])
